import numpy as np
import ml_dtypes


def mxq(x, axis, fmt="e4m3"):
    dtype, down = {"e4m3": (ml_dtypes.float8_e4m3fn, 7), "e5m2": (ml_dtypes.float8_e5m2, 14)}[fmt]
    v = np.moveaxis(np.asarray(x, np.float32).astype(ml_dtypes.bfloat16).astype(np.float64), axis, -1)
    blocks = v.reshape(v.shape[:-1] + (-1, 32))
    amax = np.abs(blocks).max(-1, keepdims=True)
    byte = np.maximum(np.where(amax > 0, np.frexp(amax)[1] - 1 + 127, 0) - down, 1)
    scale = np.exp2(byte - 127.0)
    codes = (blocks / scale).astype(np.float32).astype(dtype).astype(np.float64)
    return np.moveaxis((codes * scale).reshape(v.shape), -1, axis)


WIDE = False


def mx_kscale(k):
    if not WIDE:
        return np.ones(k)
    levels = np.array([10, -10, 5, -5, 0])
    if k % 512:
        return np.exp2(np.random.permutation(np.resize(levels, k // 32))).repeat(32)
    a = np.empty((k // 512, 16))
    for p in range(k // 512):
        a[p, :8] = np.random.permutation(np.resize(levels, 8))
        for g in range(8):
            far = levels[np.abs(levels - a[p, g]) >= 10]
            a[p, g + 8] = far[np.random.randint(len(far))]
    return np.exp2(a.ravel()).repeat(32)


def f64(x):
    return np.asarray(x).astype(np.float64)


def striped(idx):
    return np.tile(idx.reshape(-1, 16).T, (8, 1)).astype(np.uint16)


def unstriped(offs):
    return offs[:16].T.reshape(-1).astype(np.int64)


def striped8(idx):
    return np.concatenate([x.reshape(-1, 16).T for x in idx]).astype(np.uint16)


def runs(offs, k):
    lists = np.stack([offs[16 * r : 16 * r + 16].T.reshape(-1) for r in range(8)]).astype(np.int64)
    return lists[np.arange(k) % 512 // 64]


def pack_weight(w):
    k, n = w.shape
    w = f64(np.asarray(w, np.float32).astype(ml_dtypes.bfloat16)).reshape(k // 32, 32, n)
    amax = np.abs(w).max(1)
    byte = np.clip(np.where(amax > 0, np.frexp(amax)[1] - 1 + 127 - 7, 1), 1, 254)
    scaled = (w * np.exp2(127.0 - byte)[:, None, :]).reshape(k, n).astype(np.float32)
    words = np.ascontiguousarray(scaled.reshape(k // 512, 128, 4, n).transpose(0, 1, 3, 2)).astype(ml_dtypes.float8_e4m3fn).view(np.uint8)
    return words, np.ascontiguousarray(byte.astype(np.uint8).reshape(k // 512, 16, n))


def unpack_weight(words, scales):
    g, p, n, _ = words.shape
    vals = np.ascontiguousarray(words).view(ml_dtypes.float8_e4m3fn).astype(np.float64) * np.repeat(np.exp2(scales.astype(np.float64) - 127.0), 8, axis=1)[..., None]
    return vals.transpose(0, 1, 3, 2).reshape(g * 512, n)


E2M1 = np.array([0.0, 0.5, 1.0, 1.5, 2.0, 3.0, 4.0, 6.0, -0.0, -0.5, -1.0, -1.5, -2.0, -3.0, -4.0, -6.0])


def pack_fp4(w):
    k, n = w.shape
    w = f64(np.asarray(w, np.float32).astype(ml_dtypes.bfloat16)).reshape(k // 32, 32, n)
    amax = np.abs(w).max(1)
    mant, ex = np.frexp(amax / 6.0)
    byte = np.clip(np.where(amax > 0, np.where(mant > 0.5, ex, ex - 1) + 127, 1), 1, 254)
    scaled = (w * np.exp2(127.0 - byte)[:, None, :]).reshape(k, n).astype(np.float32)
    c = np.ascontiguousarray(scaled.reshape(k // 512, 128, 4, n).transpose(0, 1, 3, 2)).astype(ml_dtypes.float4_e2m1fn).view(np.uint8) & 0xF
    words = (c[..., 0::2] | (c[..., 1::2] << 4)).reshape(k // 512, 128, 2 * n)
    return np.ascontiguousarray(words), np.ascontiguousarray(byte.astype(np.uint8).reshape(k // 512, 16, n))


def unpack_fp4(words, scales):
    g, _, n = scales.shape
    words = np.ascontiguousarray(words).reshape(g, 128, n, 2)
    nib = np.empty((g, 128, n, 4), np.uint8)
    nib[..., 0::2] = words & 0xF
    nib[..., 1::2] = words >> 4
    vals = E2M1[nib] * np.repeat(np.exp2(scales.astype(np.float64) - 127.0), 8, axis=1)[..., None]
    return vals.transpose(0, 1, 3, 2).reshape(g * 512, n)


def planes(y):
    n, m = y.shape
    v = y.astype(np.float32).astype(ml_dtypes.bfloat16).astype(np.float64).reshape(n // 32, 32, m)
    top = np.abs(v).max(1)
    byte = np.clip(np.where(top > 0, np.frexp(top)[1] - 1 + 127 - 7, 1), 1, 254)
    codes = (v * np.exp2(127.0 - byte)[:, None, :]).reshape(n, m).astype(np.float32).astype(ml_dtypes.float8_e4m3fn).view(np.uint8)
    words = codes.reshape(n // 512, 128, 4, m).transpose(0, 1, 3, 2)
    return np.ascontiguousarray(words), np.ascontiguousarray(byte.astype(np.uint8).reshape(n // 512, 16, m))


K, T, S, V, N, H = 512, 2048, 512, 128, 512, 512


def setup_inputs():
    n = np.random.standard_normal
    s = mx_kscale(K)[:, None]
    u = mx_kscale(H)
    packed_xT = pack_weight(n((K, T)) * s)
    packed_w2 = pack_fp4(n((H, N)) / np.sqrt(H) / u[:, None])
    perm = np.stack([np.random.permutation(S) for _ in range(8)])
    return {
        "x_words": packed_xT[0],
        "x_scales": packed_xT[1],
        "w1": (n((K, H)) / np.sqrt(K) / s * u).astype(np.float32),
        "w2_words": packed_w2[0],
        "w2_scales": packed_w2[1],
        "offs": striped(np.random.permutation(T)[:S]),
        "la": striped8(perm[:, :V]),
        "lb": striped8(perm[:, V:2 * V]),
        "lc": striped8(perm[:, 2 * V:3 * V]),
        "ld": striped8(perm[:, 3 * V:]),
    }


def reference(x_words, x_scales, w1, w2_words, w2_scales, offs, la, lb, lc, ld):
    xq = unpack_weight(x_words, x_scales)[:, unstriped(offs)]
    y = mxq(f64(w1), 0, "e4m3").T @ xq
    b = y[np.arange(H)[:, None], runs(lb, H)]
    d = y[np.arange(H)[:, None], runs(ld, H)]
    n3 = np.minimum(b, d)
    c = y[np.arange(H)[:, None], runs(lc, H)]
    n2 = c + d
    a = y[np.arange(H)[:, None], runs(la, H)]
    n1 = np.maximum(a, b)
    n0 = a - c
    p0 = np.zeros((H, S))
    p0[np.arange(H)[:, None], runs(la, H)] = n0
    p = p0.copy()
    p[np.arange(H)[:, None], runs(lb, H)] = n1
    p2 = p.copy()
    p2[np.arange(H)[:, None], runs(lc, H)] = n2
    z = p2.copy()
    z[np.arange(H)[:, None], runs(ld, H)] = n3
    out_0 = unpack_fp4(w2_words, w2_scales).T @ mxq(z, 0, "e4m3")
    return (out_0,) + planes(out_0)

@@ -1,0 +1,232 @@
+from contextlib import ExitStack
+
+import concourse.mybir as mybir
+
+K, T, S, V, N, H = 512, 2048, 512, 128, 512, 512
+FLOPS = 2 * K * H * S + 2 * H * N * S
+
+F32 = mybir.dt.float32
+BF16 = mybir.dt.bfloat16
+I32 = mybir.dt.int32
+U32 = mybir.dt.uint32
+U16 = mybir.dt.uint16
+U8 = mybir.dt.uint8
+FP8X4 = mybir.dt.float8_e4m3fn_x4
+FP4X4 = mybir.dt.float4_e2m1fn_x4
+ALU = mybir.AluOpType
+COPY = mybir.ActivationFunctionType.Copy
+
+P = 128
+PACK = 4
+QUADS = 4
+CHUNK = 128
+CHUNKS = S // CHUNK
+HALF = S // 2
+W1_VECTOR_COLS = 80
+
+
+def tile_picked_quart4_none_po_kernel(
+    tc, x_words, x_scales, w1, w2_words, w2_scales, offs, la, lb, lc, ld, out_0, out_1, out_2
+):
+    nc = tc.nc
+    with ExitStack() as ctx:
+        lists = ctx.enter_context(tc.tile_pool(name="lists", bufs=1))
+        sb = ctx.enter_context(tc.tile_pool(name="sb", bufs=1))
+        psum = ctx.enter_context(tc.psum_pool(name="psum", bufs=1))
+
+        def load_scale_rows(engine, tile, rows):
+            for q in range(QUADS):
+                engine.dma_start(
+                    out=tile[32 * q : 32 * q + 4, :].bitcast(I32),
+                    in_=rows[4 * q : 4 * q + 4, :].bitcast(I32),
+                )
+
+        x_scale_table = sb.tile([P, T], U8, name="x_scale_table", align_bytes=64)
+        nc.vector.memset(x_scale_table[:].bitcast(I32), 0)
+        w2_scale_raw = sb.tile([P, N], U8, name="w2_scale_raw", align_bytes=64)
+        nc.gpsimd.memset(w2_scale_raw[:].bitcast(I32), 0)
+
+        def load_list(name, source):
+            tile = lists.tile([P, source.shape[1]], U16, name=name)
+            nc.sync.dma_start(tile[:], source)
+            return tile
+
+        offs_t = load_list("offs_t", offs)
+        lc_t = load_list("lc_t", lc)
+        ld_t = load_list("ld_t", ld)
+        lb_t = load_list("lb_t", lb)
+        w1_raw = sb.tile([P, PACK, H], F32, name="w1_raw", align_bytes=64)
+        nc.sync.dma_start(out=w1_raw[:], in_=w1.rearrange("(p j) c -> p j c", j=PACK))
+        x_table = sb.tile([P, T], U32, name="x_table", tag="x_table", align_bytes=64)
+        nc.sync.dma_start(out=x_table[:].bitcast(I32), in_=x_words[0].rearrange("p n t -> p (n t)").bitcast(I32))
+        load_scale_rows(nc.scalar, x_scale_table, x_scales[0])
+        w2_raw = sb.tile([P, 2 * N], U8, name="w2_raw", tag="w2_raw", align_bytes=64)
+        nc.sync.dma_start(out=w2_raw[:].bitcast(I32), in_=w2_words[0].bitcast(I32))
+        la_t = load_list("la_t", la)
+        load_scale_rows(nc.gpsimd, w2_scale_raw, w2_scales[0])
+
+        x_scale_picked = sb.tile([P, S], U8, name="x_scale_picked", align_bytes=64)
+        nc.vector.tensor_copy(x_scale_picked[:], x_scale_table[:].indirect(offs_t[:]))
+
+        w1_bf = sb.tile([P, PACK * H], BF16, name="w1_bf", align_bytes=64)
+        dealt = w1_bf[:].rearrange("p (t m j) -> p m t j", t=PACK, j=PACK)
+        source = w1_raw[:].rearrange("p j (m t) -> p m t j", t=PACK)
+        nc.vector.tensor_copy(out=dealt[:, :W1_VECTOR_COLS], in_=source[:, :W1_VECTOR_COLS])
+        nc.scalar.activation(dealt[:, W1_VECTOR_COLS:], source[:, W1_VECTOR_COLS:], COPY)
+        w1_codes = sb.tile([P, H], U32, name="w1_codes", align_bytes=64)
+        w1_scales = sb.tile([P, H], U8, name="w1_scales", align_bytes=64)
+        nc.vector.quantize_mx(out=w1_codes[:].bitcast(FP8X4), scales=w1_scales[:], in_=w1_bf[:])
+
+        x_picked = sb.tile([P, S], U32, name="x_picked", align_bytes=64)
+        for h in range(2):
+            nc.vector.tensor_copy(
+                x_picked[:, h * HALF : (h + 1) * HALF],
+                x_table[:].indirect(offs_t[:, h * HALF // 16 : (h + 1) * HALF // 16]),
+            )
+
+        y = [sb.tile([P, S], F32, name="y%d" % t, align_bytes=64) for t in range(PACK)]
+
+        def first_product(t, cols, tag):
+            rows = slice(t * P, (t + 1) * P)
+            bank = psum.tile([P, cols.stop - cols.start], F32, name="bank_" + tag, tag=tag)
+            nc.tensor.matmul_mx(
+                out=bank[:],
+                lhsT=w1_codes[:, rows].bitcast(FP8X4),
+                lhsT_scale=w1_scales[:, rows],
+                rhs=x_picked[:, cols].bitcast(FP8X4),
+                rhs_scale=x_scale_picked[:, cols],
+                start=True,
+                stop=True,
+            )
+            nc.scalar.copy(y[t][:, cols], bank[:])
+
+        first_product(0, slice(0, HALF), "b0")
+        first_product(0, slice(HALF, S), "b1")
+        for t in range(1, PACK):
+            first_product(t, slice(0, S), "b%d" % (t + 1))
+
+        w2_codes = sb.tile([P, 2 * N], U8, name="w2_codes", tag="x_table", align_bytes=64)
+        nc.vector.tensor_copy(
+            out=w2_codes[:].rearrange("p (t m b) -> p t m b", t=PACK, b=2),
+            in_=w2_raw[:].rearrange("p (m t b) -> p t m b", t=PACK, b=2),
+        )
+        w2_scale = sb.tile([P, N], U8, name="w2_scale", tag="w2_raw", align_bytes=64)
+        nc.vector.tensor_copy(
+            out=w2_scale[:].rearrange("p (t m) -> p t m", t=PACK),
+            in_=w2_scale_raw[:].rearrange("p (m t) -> p t m", t=PACK),
+        )
+
+        def small(name, t):
+            return sb.tile([P, V], F32, name="%s%d" % (name, t), align_bytes=64)
+
+        a = [small("a", t) for t in range(PACK)]
+        b = [small("b", t) for t in range(PACK)]
+        c = [small("c", t) for t in range(PACK)]
+        d = [small("d", t) for t in range(PACK)]
+        minus_c = [small("minus_c", t) for t in range(PACK)]
+        larger = [small("larger", t) for t in range(PACK)]
+        smaller = [small("smaller", t) for t in range(PACK)]
+        z = [sb.tile([P, S], F32, name="z%d" % t, align_bytes=64) for t in range(PACK)]
+        z_bf = [sb.tile([P, CHUNK, PACK], BF16, name="z_bf%d" % i, align_bytes=64) for i in range(CHUNKS)]
+
+        def gathers(t):
+            return [
+                lambda: nc.vector.tensor_copy(c[t][:], y[t][:].indirect(lc_t[:])),
+                lambda: nc.vector.tensor_copy(d[t][:], y[t][:].indirect(ld_t[:])),
+                lambda: nc.vector.tensor_copy(b[t][:], y[t][:].indirect(lb_t[:])),
+                lambda: nc.vector.tensor_copy(a[t][:], y[t][:].indirect(la_t[:])),
+            ]
+
+        def scatters(t):
+            return [
+                lambda: nc.vector.tensor_tensor(z[t][:].indirect(lc_t[:]), c[t][:], d[t][:], ALU.add),
+                lambda: nc.vector.tensor_copy(z[t][:].indirect(ld_t[:]), smaller[t][:]),
+                lambda: nc.vector.tensor_copy(z[t][:].indirect(lb_t[:]), larger[t][:]),
+                lambda: nc.vector.tensor_tensor(z[t][:].indirect(la_t[:]), a[t][:], minus_c[t][:], ALU.add),
+            ]
+
+        def round_z(t, i, on_vector):
+            src = z[t][:, i * CHUNK : (i + 1) * CHUNK]
+            if on_vector:
+                nc.vector.tensor_copy(z_bf[i][:, :, t], src)
+            else:
+                nc.scalar.copy(z_bf[i][:, :, t], src)
+
+        for t in range(PACK):
+            put = scatters(t - 1) if t > 0 else None
+            for k, fetch in enumerate(gathers(t)):
+                fetch()
+                if k == 0:
+                    nc.scalar.activation(minus_c[t][:], c[t][:], COPY, scale=-1.0)
+                if put:
+                    put[k]()
+            nc.vector.tensor_tensor(smaller[t][:], b[t][:], d[t][:], ALU.min)
+            nc.vector.tensor_tensor(larger[t][:], a[t][:], b[t][:], ALU.max)
+            if t in (1, 2):
+                for i in range(CHUNKS):
+                    round_z(t - 1, i, False)
+        last = scatters(PACK - 1)
+        round_z(2, 2, False)
+        round_z(2, 3, False)
+        last[0]()
+        round_z(2, 0, True)
+        last[1]()
+        round_z(2, 1, True)
+        last[2]()
+        last[3]()
+        for i in range(CHUNKS):
+            round_z(3, i, i < 2)
+
+        z_codes = sb.tile([P, S], U32, name="z_codes", align_bytes=64)
+        z_scales = sb.tile([P, S], U8, name="z_scales", align_bytes=64)
+        for i in range(CHUNKS):
+            cols = slice(i * CHUNK, (i + 1) * CHUNK)
+            nc.vector.quantize_mx(
+                out=z_codes[:, cols].bitcast(FP8X4),
+                scales=z_scales[:, cols],
+                in_=z_bf[i][:].rearrange("p n t -> p (n t)"),
+            )
+
+        out_rows = out_0.rearrange("(p t) n -> p t n", t=PACK)
+        out_words = out_1[0].rearrange("p n t -> p (n t)").bitcast(I32)
+        out_codes = sb.tile([P, S], U32, name="out_codes", align_bytes=64)
+        out_scales = sb.tile([P, S], U8, name="out_scales", align_bytes=64)
+        out_tags = ["b5", "b6", "b7", "b0"]
+        for i in range(CHUNKS):
+            cols = slice(i * CHUNK, (i + 1) * CHUNK)
+            bank = psum.tile([P, PACK, CHUNK], F32, name="out_bank%d" % i, tag=out_tags[i])
+            for t in range(PACK):
+                nc.tensor.matmul_mx(
+                    out=bank[:, t, :],
+                    lhsT=w2_codes[:, 2 * t * P : 2 * (t + 1) * P].bitcast(FP4X4),
+                    lhsT_scale=w2_scale[:, t * P : (t + 1) * P],
+                    rhs=z_codes[:, cols].bitcast(FP8X4),
+                    rhs_scale=z_scales[:, cols],
+                    start=True,
+                    stop=True,
+                )
+            result = sb.tile([P, PACK, CHUNK], F32, name="result%d" % i, align_bytes=64)
+            result_bf = sb.tile([P, CHUNK, PACK], BF16, name="result_bf%d" % i, align_bytes=64)
+            if i == CHUNKS - 1:
+                nc.vector.tensor_copy(out=result_bf[:], in_=bank[:].rearrange("p t n -> p n t"))
+            nc.scalar.copy(result[:], bank[:])
+            nc.sync.dma_start(out=out_rows[:, :, cols], in_=result[:])
+            if i < CHUNKS - 1:
+                nc.vector.tensor_copy(
+                    out=result_bf[:].rearrange("p (n i) t -> p n t i", i=4),
+                    in_=result[:].rearrange("p t (n i) -> p n t i", i=4),
+                )
+            nc.vector.quantize_mx(
+                out=out_codes[:, cols].bitcast(FP8X4),
+                scales=out_scales[:, cols],
+                in_=result_bf[:].rearrange("p n t -> p (n t)"),
+            )
+            if i % 2 == 1:
+                half = slice((i - 1) * CHUNK, (i + 1) * CHUNK)
+                nc.sync.dma_start(out=out_words[:, half], in_=out_codes[:, half].bitcast(I32))
+        for q in range(QUADS):
+            engine = nc.sync if q % 2 == 0 else nc.scalar
+            engine.dma_start(
+                out=out_2[0][4 * q : 4 * q + 4, :].bitcast(I32),
+                in_=out_scales[32 * q : 32 * q + 4, :].bitcast(I32),
+            )

@@ -41,10 +41,8 @@ def tile_picked_quart4_none_po_kernel(
                     in_=rows[4 * q : 4 * q + 4, :].bitcast(I32),
                 )
 
-        x_scale_table = sb.tile([P, T], U8, name="x_scale_table", align_bytes=64)
+        x_scale_table = sb.tile([P, T], U8, name="x_scale_table", tag="x_scale_table", align_bytes=64)
         nc.vector.memset(x_scale_table[:].bitcast(I32), 0)
-        w2_scale_raw = sb.tile([P, N], U8, name="w2_scale_raw", align_bytes=64)
-        nc.gpsimd.memset(w2_scale_raw[:].bitcast(I32), 0)
 
         def load_list(name, source):
             tile = lists.tile([P, source.shape[1]], U16, name=name)
@@ -54,16 +52,13 @@ def tile_picked_quart4_none_po_kernel(
         offs_t = load_list("offs_t", offs)
         lc_t = load_list("lc_t", lc)
         ld_t = load_list("ld_t", ld)
-        lb_t = load_list("lb_t", lb)
-        w1_raw = sb.tile([P, PACK, H], F32, name="w1_raw", align_bytes=64)
+        w1_raw = sb.tile([P, PACK, H], F32, name="w1_raw", tag="w1_raw", align_bytes=64)
         nc.sync.dma_start(out=w1_raw[:], in_=w1.rearrange("(p j) c -> p j c", j=PACK))
+        load_scale_rows(nc.scalar, x_scale_table, x_scales[0])
         x_table = sb.tile([P, T], U32, name="x_table", tag="x_table", align_bytes=64)
         nc.sync.dma_start(out=x_table[:].bitcast(I32), in_=x_words[0].rearrange("p n t -> p (n t)").bitcast(I32))
-        load_scale_rows(nc.scalar, x_scale_table, x_scales[0])
-        w2_raw = sb.tile([P, 2 * N], U8, name="w2_raw", tag="w2_raw", align_bytes=64)
-        nc.sync.dma_start(out=w2_raw[:].bitcast(I32), in_=w2_words[0].bitcast(I32))
+        lb_t = load_list("lb_t", lb)
         la_t = load_list("la_t", la)
-        load_scale_rows(nc.gpsimd, w2_scale_raw, w2_scales[0])
 
         x_scale_picked = sb.tile([P, S], U8, name="x_scale_picked", align_bytes=64)
         nc.vector.tensor_copy(x_scale_picked[:], x_scale_table[:].indirect(offs_t[:]))
@@ -76,6 +71,12 @@ def tile_picked_quart4_none_po_kernel(
         w1_codes = sb.tile([P, H], U32, name="w1_codes", align_bytes=64)
         w1_scales = sb.tile([P, H], U8, name="w1_scales", align_bytes=64)
         nc.vector.quantize_mx(out=w1_codes[:].bitcast(FP8X4), scales=w1_scales[:], in_=w1_bf[:])
+
+        w2_raw = sb.tile([P, 2 * N], U8, name="w2_raw", tag="w1_raw", align_bytes=64)
+        nc.sync.dma_start(out=w2_raw[:].bitcast(I32), in_=w2_words[0].bitcast(I32))
+        w2_scale_raw = sb.tile([P, N], U8, name="w2_scale_raw", tag="x_scale_table", align_bytes=64)
+        nc.gpsimd.memset(w2_scale_raw[:].bitcast(I32), 0)
+        load_scale_rows(nc.sync, w2_scale_raw, w2_scales[0])
 
         x_picked = sb.tile([P, S], U32, name="x_picked", align_bytes=64)
         for h in range(2):
@@ -110,14 +111,9 @@ def tile_picked_quart4_none_po_kernel(
             out=w2_codes[:].rearrange("p (t m b) -> p t m b", t=PACK, b=2),
             in_=w2_raw[:].rearrange("p (m t b) -> p t m b", t=PACK, b=2),
         )
-        w2_scale = sb.tile([P, N], U8, name="w2_scale", tag="w2_raw", align_bytes=64)
-        nc.vector.tensor_copy(
-            out=w2_scale[:].rearrange("p (t m) -> p t m", t=PACK),
-            in_=w2_scale_raw[:].rearrange("p (m t) -> p t m", t=PACK),
-        )
 
         def small(name, t):
-            return sb.tile([P, V], F32, name="%s%d" % (name, t), align_bytes=64)
+            return sb.tile([P, V], F32, name="%s%d" % (name, t), tag="%s%d" % (name, t), align_bytes=64)
 
         a = [small("a", t) for t in range(PACK)]
         b = [small("b", t) for t in range(PACK)]
@@ -173,6 +169,11 @@ def tile_picked_quart4_none_po_kernel(
         last[1]()
         round_z(2, 1, True)
         last[2]()
+        w2_scale = sb.tile([P, N], U8, name="w2_scale", tag="smaller3", align_bytes=64)
+        nc.vector.tensor_copy(
+            out=w2_scale[:].rearrange("p (t m) -> p t m", t=PACK),
+            in_=w2_scale_raw[:].rearrange("p (m t) -> p t m", t=PACK),
+        )
         last[3]()
         for i in range(CHUNKS):
             round_z(3, i, i < 2)
@@ -191,39 +192,38 @@ def tile_picked_quart4_none_po_kernel(
         out_words = out_1[0].rearrange("p n t -> p (n t)").bitcast(I32)
         out_codes = sb.tile([P, S], U32, name="out_codes", align_bytes=64)
         out_scales = sb.tile([P, S], U8, name="out_scales", align_bytes=64)
-        out_tags = ["b5", "b6", "b7", "b0"]
         for i in range(CHUNKS):
             cols = slice(i * CHUNK, (i + 1) * CHUNK)
-            bank = psum.tile([P, PACK, CHUNK], F32, name="out_bank%d" % i, tag=out_tags[i])
-            for t in range(PACK):
-                nc.tensor.matmul_mx(
-                    out=bank[:, t, :],
-                    lhsT=w2_codes[:, 2 * t * P : 2 * (t + 1) * P].bitcast(FP4X4),
-                    lhsT_scale=w2_scale[:, t * P : (t + 1) * P],
-                    rhs=z_codes[:, cols].bitcast(FP8X4),
-                    rhs_scale=z_scales[:, cols],
-                    start=True,
-                    stop=True,
-                )
             result = sb.tile([P, PACK, CHUNK], F32, name="result%d" % i, align_bytes=64)
-            result_bf = sb.tile([P, CHUNK, PACK], BF16, name="result_bf%d" % i, align_bytes=64)
-            if i == CHUNKS - 1:
-                nc.vector.tensor_copy(out=result_bf[:], in_=bank[:].rearrange("p t n -> p n t"))
-            nc.scalar.copy(result[:], bank[:])
+            for u in range(2):
+                tag = "b%d" % ((2 * i + u + 5) % 8)
+                bank = psum.tile([P, 2, CHUNK], F32, name="out_bank%d_%d" % (i, u), tag=tag)
+                for e in range(2):
+                    t = 2 * u + e
+                    nc.tensor.matmul_mx(
+                        out=bank[:, e, :],
+                        lhsT=w2_codes[:, 2 * t * P : 2 * (t + 1) * P].bitcast(FP4X4),
+                        lhsT_scale=w2_scale[:, t * P : (t + 1) * P],
+                        rhs=z_codes[:, cols].bitcast(FP8X4),
+                        rhs_scale=z_scales[:, cols],
+                        start=True,
+                        stop=True,
+                    )
+                nc.scalar.copy(result[:, 2 * u : 2 * u + 2, :], bank[:])
             nc.sync.dma_start(out=out_rows[:, :, cols], in_=result[:])
-            if i < CHUNKS - 1:
-                nc.vector.tensor_copy(
-                    out=result_bf[:].rearrange("p (n i) t -> p n t i", i=4),
-                    in_=result[:].rearrange("p t (n i) -> p n t i", i=4),
-                )
+            result_bf = sb.tile([P, CHUNK, PACK], BF16, name="result_bf%d" % i, align_bytes=64)
+            nc.vector.tensor_copy(
+                out=result_bf[:].rearrange("p (n i) t -> p n t i", i=4),
+                in_=result[:].rearrange("p t (n i) -> p n t i", i=4),
+            )
             nc.vector.quantize_mx(
                 out=out_codes[:, cols].bitcast(FP8X4),
                 scales=out_scales[:, cols],
                 in_=result_bf[:].rearrange("p n t -> p (n t)"),
             )
-            if i % 2 == 1:
-                half = slice((i - 1) * CHUNK, (i + 1) * CHUNK)
-                nc.sync.dma_start(out=out_words[:, half], in_=out_codes[:, half].bitcast(I32))
+            if i >= CHUNKS - 2:
+                done = slice(0, (i + 1) * CHUNK) if i == CHUNKS - 2 else cols
+                nc.sync.dma_start(out=out_words[:, done], in_=out_codes[:, done].bitcast(I32))
         for q in range(QUADS):
             engine = nc.sync if q % 2 == 0 else nc.scalar
             engine.dma_start(

@@ -22,7 +22,6 @@ QUADS = 4
 CHUNK = 128
 CHUNKS = S // CHUNK
 HALF = S // 2
-W1_VECTOR_COLS = 80
 
 
 def tile_picked_quart4_none_po_kernel(
@@ -32,6 +31,7 @@ def tile_picked_quart4_none_po_kernel(
     with ExitStack() as ctx:
         lists = ctx.enter_context(tc.tile_pool(name="lists", bufs=1))
         sb = ctx.enter_context(tc.tile_pool(name="sb", bufs=1))
+        shared = ctx.enter_context(tc.tile_pool(name="shared", bufs=1))
         psum = ctx.enter_context(tc.psum_pool(name="psum", bufs=1))
 
         def load_scale_rows(engine, tile, rows):
@@ -41,7 +41,7 @@ def tile_picked_quart4_none_po_kernel(
                     in_=rows[4 * q : 4 * q + 4, :].bitcast(I32),
                 )
 
-        x_scale_table = sb.tile([P, T], U8, name="x_scale_table", tag="x_scale_table", align_bytes=64)
+        x_scale_table = shared.tile([P, T], U8, name="x_scale_table", offset=0, align_bytes=64)
         nc.vector.memset(x_scale_table[:].bitcast(I32), 0)
 
         def load_list(name, source):
@@ -55,7 +55,7 @@ def tile_picked_quart4_none_po_kernel(
         w1_raw = sb.tile([P, PACK, H], F32, name="w1_raw", tag="w1_raw", align_bytes=64)
         nc.sync.dma_start(out=w1_raw[:], in_=w1.rearrange("(p j) c -> p j c", j=PACK))
         load_scale_rows(nc.scalar, x_scale_table, x_scales[0])
-        x_table = sb.tile([P, T], U32, name="x_table", tag="x_table", align_bytes=64)
+        x_table = shared.tile([P, T], U32, name="x_table", offset=4096, align_bytes=64)
         nc.sync.dma_start(out=x_table[:].bitcast(I32), in_=x_words[0].rearrange("p n t -> p (n t)").bitcast(I32))
         lb_t = load_list("lb_t", lb)
         la_t = load_list("la_t", la)
@@ -63,37 +63,42 @@ def tile_picked_quart4_none_po_kernel(
         x_scale_picked = sb.tile([P, S], U8, name="x_scale_picked", align_bytes=64)
         nc.vector.tensor_copy(x_scale_picked[:], x_scale_table[:].indirect(offs_t[:]))
 
-        w1_bf = sb.tile([P, PACK * H], BF16, name="w1_bf", align_bytes=64)
-        dealt = w1_bf[:].rearrange("p (t m j) -> p m t j", t=PACK, j=PACK)
+        w1_bf = [
+            shared.tile([P, 2 * PACK * P], BF16, name="w1_bf_early", offset=2048, align_bytes=64),
+            sb.tile([P, 2 * PACK * P], BF16, name="w1_bf_late", tag="w1_bf_late", align_bytes=64),
+        ]
         source = w1_raw[:].rearrange("p j (m t) -> p m t j", t=PACK)
-        nc.vector.tensor_copy(out=dealt[:, :W1_VECTOR_COLS], in_=source[:, :W1_VECTOR_COLS])
-        nc.scalar.activation(dealt[:, W1_VECTOR_COLS:], source[:, W1_VECTOR_COLS:], COPY)
-        w1_codes = sb.tile([P, H], U32, name="w1_codes", align_bytes=64)
-        w1_scales = sb.tile([P, H], U8, name="w1_scales", align_bytes=64)
-        nc.vector.quantize_mx(out=w1_codes[:].bitcast(FP8X4), scales=w1_scales[:], in_=w1_bf[:])
+        dealt = [tile[:].rearrange("p (t m j) -> p m t j", t=2, j=PACK) for tile in w1_bf]
+        nc.vector.tensor_copy(out=dealt[0], in_=source[:, :, 0:2, :])
+        nc.scalar.activation(dealt[1], source[:, :, 2:4, :], COPY)
+        w1_codes = [
+            sb.tile([P, 2 * P], U32, name="w1_codes_early", align_bytes=64),
+            shared.tile([P, 2 * P], U32, name="w1_codes_late", offset=4096 + 1024, align_bytes=64),
+        ]
+        w1_scales = [sb.tile([P, 2 * P], U8, name="w1_scales%d" % u, align_bytes=64) for u in range(2)]
+        nc.vector.quantize_mx(out=w1_codes[0][:].bitcast(FP8X4), scales=w1_scales[0][:], in_=w1_bf[0][:])
 
         w2_raw = sb.tile([P, 2 * N], U8, name="w2_raw", tag="w1_raw", align_bytes=64)
         nc.sync.dma_start(out=w2_raw[:].bitcast(I32), in_=w2_words[0].bitcast(I32))
-        w2_scale_raw = sb.tile([P, N], U8, name="w2_scale_raw", tag="x_scale_table", align_bytes=64)
-        nc.gpsimd.memset(w2_scale_raw[:].bitcast(I32), 0)
-        load_scale_rows(nc.sync, w2_scale_raw, w2_scales[0])
 
-        x_picked = sb.tile([P, S], U32, name="x_picked", align_bytes=64)
+        x_picked = shared.tile([P, S], U32, name="x_picked", offset=1024, align_bytes=64)
         for h in range(2):
             nc.vector.tensor_copy(
                 x_picked[:, h * HALF : (h + 1) * HALF],
                 x_table[:].indirect(offs_t[:, h * HALF // 16 : (h + 1) * HALF // 16]),
             )
 
+        nc.vector.quantize_mx(out=w1_codes[1][:].bitcast(FP8X4), scales=w1_scales[1][:], in_=w1_bf[1][:])
+
         y = [sb.tile([P, S], F32, name="y%d" % t, align_bytes=64) for t in range(PACK)]
 
         def first_product(t, cols, tag):
-            rows = slice(t * P, (t + 1) * P)
+            rows = slice(t % 2 * P, (t % 2 + 1) * P)
             bank = psum.tile([P, cols.stop - cols.start], F32, name="bank_" + tag, tag=tag)
             nc.tensor.matmul_mx(
                 out=bank[:],
-                lhsT=w1_codes[:, rows].bitcast(FP8X4),
-                lhsT_scale=w1_scales[:, rows],
+                lhsT=w1_codes[t // 2][:, rows].bitcast(FP8X4),
+                lhsT_scale=w1_scales[t // 2][:, rows],
                 rhs=x_picked[:, cols].bitcast(FP8X4),
                 rhs_scale=x_scale_picked[:, cols],
                 start=True,
@@ -106,7 +111,10 @@ def tile_picked_quart4_none_po_kernel(
         for t in range(1, PACK):
             first_product(t, slice(0, S), "b%d" % (t + 1))
 
-        w2_codes = sb.tile([P, 2 * N], U8, name="w2_codes", tag="x_table", align_bytes=64)
+        w2_scale_raw = sb.tile([P, N], U8, name="w2_scale_raw", tag="w1_bf_late", align_bytes=64)
+        nc.gpsimd.memset(w2_scale_raw[:].bitcast(I32), 0)
+        load_scale_rows(nc.sync, w2_scale_raw, w2_scales[0])
+        w2_codes = shared.tile([P, 2 * N], U8, name="w2_codes", offset=4096, align_bytes=64)
         nc.vector.tensor_copy(
             out=w2_codes[:].rearrange("p (t m b) -> p t m b", t=PACK, b=2),
             in_=w2_raw[:].rearrange("p (m t b) -> p t m b", t=PACK, b=2),
@@ -115,10 +123,8 @@ def tile_picked_quart4_none_po_kernel(
         def small(name, t):
             return sb.tile([P, V], F32, name="%s%d" % (name, t), tag="%s%d" % (name, t), align_bytes=64)
 
-        a = [small("a", t) for t in range(PACK)]
-        b = [small("b", t) for t in range(PACK)]
-        c = [small("c", t) for t in range(PACK)]
-        d = [small("d", t) for t in range(PACK)]
+        fetched = sb.tile([P, 4 * PACK * V], F32, name="fetched", tag="w1_raw", align_bytes=64)
+        a, b, c, d = ([fetched[:, (4 * t + k) * V : (4 * t + k + 1) * V] for t in range(PACK)] for k in range(4))
         minus_c = [small("minus_c", t) for t in range(PACK)]
         larger = [small("larger", t) for t in range(PACK)]
         smaller = [small("smaller", t) for t in range(PACK)]
@@ -127,18 +133,18 @@ def tile_picked_quart4_none_po_kernel(
 
         def gathers(t):
             return [
-                lambda: nc.vector.tensor_copy(c[t][:], y[t][:].indirect(lc_t[:])),
-                lambda: nc.vector.tensor_copy(d[t][:], y[t][:].indirect(ld_t[:])),
-                lambda: nc.vector.tensor_copy(b[t][:], y[t][:].indirect(lb_t[:])),
-                lambda: nc.vector.tensor_copy(a[t][:], y[t][:].indirect(la_t[:])),
+                lambda: nc.vector.tensor_copy(c[t], y[t][:].indirect(lc_t[:])),
+                lambda: nc.vector.tensor_copy(d[t], y[t][:].indirect(ld_t[:])),
+                lambda: nc.vector.tensor_copy(b[t], y[t][:].indirect(lb_t[:])),
+                lambda: nc.vector.tensor_copy(a[t], y[t][:].indirect(la_t[:])),
             ]
 
         def scatters(t):
             return [
-                lambda: nc.vector.tensor_tensor(z[t][:].indirect(lc_t[:]), c[t][:], d[t][:], ALU.add),
+                lambda: nc.vector.tensor_tensor(z[t][:].indirect(lc_t[:]), c[t], d[t], ALU.add),
                 lambda: nc.vector.tensor_copy(z[t][:].indirect(ld_t[:]), smaller[t][:]),
                 lambda: nc.vector.tensor_copy(z[t][:].indirect(lb_t[:]), larger[t][:]),
-                lambda: nc.vector.tensor_tensor(z[t][:].indirect(la_t[:]), a[t][:], minus_c[t][:], ALU.add),
+                lambda: nc.vector.tensor_tensor(z[t][:].indirect(la_t[:]), a[t], minus_c[t][:], ALU.add),
             ]
 
         def round_z(t, i, on_vector):
@@ -153,11 +159,11 @@ def tile_picked_quart4_none_po_kernel(
             for k, fetch in enumerate(gathers(t)):
                 fetch()
                 if k == 0:
-                    nc.scalar.activation(minus_c[t][:], c[t][:], COPY, scale=-1.0)
+                    nc.scalar.activation(minus_c[t][:], c[t], COPY, scale=-1.0)
                 if put:
                     put[k]()
-            nc.vector.tensor_tensor(smaller[t][:], b[t][:], d[t][:], ALU.min)
-            nc.vector.tensor_tensor(larger[t][:], a[t][:], b[t][:], ALU.max)
+            nc.vector.tensor_tensor(smaller[t][:], b[t], d[t], ALU.min)
+            nc.vector.tensor_tensor(larger[t][:], a[t], b[t], ALU.max)
             if t in (1, 2):
                 for i in range(CHUNKS):
                     round_z(t - 1, i, False)
@@ -174,6 +180,17 @@ def tile_picked_quart4_none_po_kernel(
             out=w2_scale[:].rearrange("p (t m) -> p t m", t=PACK),
             in_=w2_scale_raw[:].rearrange("p (m t) -> p t m", t=PACK),
         )
+        warm = psum.tile([P, S], F32, name="warm", tag="b4")
+        for t in range(2):
+            nc.tensor.matmul_mx(
+                out=warm[:],
+                lhsT=w2_codes[:, 2 * t * P : 2 * (t + 1) * P].bitcast(FP4X4),
+                lhsT_scale=w2_scale[:, t * P : (t + 1) * P],
+                rhs=x_picked[:].bitcast(FP8X4),
+                rhs_scale=x_scale_picked[:],
+                start=True,
+                stop=True,
+            )
         last[3]()
         for i in range(CHUNKS):
             round_z(3, i, i < 2)
@@ -192,6 +209,14 @@ def tile_picked_quart4_none_po_kernel(
         out_words = out_1[0].rearrange("p n t -> p (n t)").bitcast(I32)
         out_codes = sb.tile([P, S], U32, name="out_codes", align_bytes=64)
         out_scales = sb.tile([P, S], U8, name="out_scales", align_bytes=64)
+        first_half = sb.tile([P, HALF * PACK], BF16, name="first_half", align_bytes=64)
+        third = sb.tile([P, CHUNK * PACK], BF16, name="third", align_bytes=64)
+        fourth = sb.tile([P, CHUNK * PACK], BF16, name="fourth", align_bytes=64)
+        result_bf = [first_half[:, : CHUNK * PACK], first_half[:, CHUNK * PACK :], third[:], fourth[:]]
+
+        def quantize_result(values, cols):
+            nc.vector.quantize_mx(out=out_codes[:, cols].bitcast(FP8X4), scales=out_scales[:, cols], in_=values)
+
         for i in range(CHUNKS):
             cols = slice(i * CHUNK, (i + 1) * CHUNK)
             result = sb.tile([P, PACK, CHUNK], F32, name="result%d" % i, align_bytes=64)
@@ -209,21 +234,25 @@ def tile_picked_quart4_none_po_kernel(
                         start=True,
                         stop=True,
                     )
-                nc.scalar.copy(result[:, 2 * u : 2 * u + 2, :], bank[:])
-            nc.sync.dma_start(out=out_rows[:, :, cols], in_=result[:])
-            result_bf = sb.tile([P, CHUNK, PACK], BF16, name="result_bf%d" % i, align_bytes=64)
+                pair = slice(2 * u, 2 * u + 2)
+                if (i, u) == (0, 1):
+                    nc.vector.tensor_copy(result[:, pair, :], bank[:])
+                else:
+                    nc.scalar.copy(result[:, pair, :], bank[:])
+                if i == 0:
+                    nc.sync.dma_start(out=out_rows[:, pair, cols], in_=result[:, pair, :])
+            if i > 0:
+                nc.sync.dma_start(out=out_rows[:, :, cols], in_=result[:])
             nc.vector.tensor_copy(
-                out=result_bf[:].rearrange("p (n i) t -> p n t i", i=4),
+                out=result_bf[i].rearrange("p (n i t) -> p n t i", i=4, t=PACK),
                 in_=result[:].rearrange("p t (n i) -> p n t i", i=4),
             )
-            nc.vector.quantize_mx(
-                out=out_codes[:, cols].bitcast(FP8X4),
-                scales=out_scales[:, cols],
-                in_=result_bf[:].rearrange("p n t -> p (n t)"),
-            )
-            if i >= CHUNKS - 2:
-                done = slice(0, (i + 1) * CHUNK) if i == CHUNKS - 2 else cols
-                nc.sync.dma_start(out=out_words[:, done], in_=out_codes[:, done].bitcast(I32))
+            if i == 2:
+                quantize_result(first_half[:], slice(0, HALF))
+        for i in (2, 3):
+            quantize_result(result_bf[i], slice(i * CHUNK, (i + 1) * CHUNK))
+        for cols in (slice(0, 3 * CHUNK), slice(3 * CHUNK, S)):
+            nc.sync.dma_start(out=out_words[:, cols], in_=out_codes[:, cols].bitcast(I32))
         for q in range(QUADS):
             engine = nc.sync if q % 2 == 0 else nc.scalar
             engine.dma_start(

@@ -180,17 +180,6 @@ def tile_picked_quart4_none_po_kernel(
             out=w2_scale[:].rearrange("p (t m) -> p t m", t=PACK),
             in_=w2_scale_raw[:].rearrange("p (m t) -> p t m", t=PACK),
         )
-        warm = psum.tile([P, S], F32, name="warm", tag="b4")
-        for t in range(2):
-            nc.tensor.matmul_mx(
-                out=warm[:],
-                lhsT=w2_codes[:, 2 * t * P : 2 * (t + 1) * P].bitcast(FP4X4),
-                lhsT_scale=w2_scale[:, t * P : (t + 1) * P],
-                rhs=x_picked[:].bitcast(FP8X4),
-                rhs_scale=x_scale_picked[:],
-                start=True,
-                stop=True,
-            )
         last[3]()
         for i in range(CHUNKS):
             round_z(3, i, i < 2)

from contextlib import ExitStack

import concourse.mybir as mybir

K, T, S, V, N, H = 512, 2048, 512, 128, 512, 512
FLOPS = 2 * K * H * S + 2 * H * N * S

F32 = mybir.dt.float32
BF16 = mybir.dt.bfloat16
I32 = mybir.dt.int32
U32 = mybir.dt.uint32
U16 = mybir.dt.uint16
U8 = mybir.dt.uint8
FP8X4 = mybir.dt.float8_e4m3fn_x4
FP4X4 = mybir.dt.float4_e2m1fn_x4
ALU = mybir.AluOpType
COPY = mybir.ActivationFunctionType.Copy

P = 128
PACK = 4
QUADS = 4
CHUNK = 128
CHUNKS = S // CHUNK
HALF = S // 2


def tile_picked_quart4_none_po_kernel(
    tc, x_words, x_scales, w1, w2_words, w2_scales, offs, la, lb, lc, ld, out_0, out_1, out_2
):
    nc = tc.nc
    with ExitStack() as ctx:
        lists = ctx.enter_context(tc.tile_pool(name="lists", bufs=1))
        sb = ctx.enter_context(tc.tile_pool(name="sb", bufs=1))
        shared = ctx.enter_context(tc.tile_pool(name="shared", bufs=1))
        psum = ctx.enter_context(tc.psum_pool(name="psum", bufs=1))

        def load_scale_rows(engine, tile, rows):
            for q in range(QUADS):
                engine.dma_start(
                    out=tile[32 * q : 32 * q + 4, :].bitcast(I32),
                    in_=rows[4 * q : 4 * q + 4, :].bitcast(I32),
                )

        x_scale_table = shared.tile([P, T], U8, name="x_scale_table", offset=0, align_bytes=64)
        nc.vector.memset(x_scale_table[:].bitcast(I32), 0)

        def load_list(name, source):
            tile = lists.tile([P, source.shape[1]], U16, name=name)
            nc.sync.dma_start(tile[:], source)
            return tile

        offs_t = load_list("offs_t", offs)
        lc_t = load_list("lc_t", lc)
        ld_t = load_list("ld_t", ld)
        w1_raw = sb.tile([P, PACK, H], F32, name="w1_raw", tag="w1_raw", align_bytes=64)
        nc.sync.dma_start(out=w1_raw[:], in_=w1.rearrange("(p j) c -> p j c", j=PACK))
        load_scale_rows(nc.scalar, x_scale_table, x_scales[0])
        x_table = shared.tile([P, T], U32, name="x_table", offset=4096, align_bytes=64)
        nc.sync.dma_start(out=x_table[:].bitcast(I32), in_=x_words[0].rearrange("p n t -> p (n t)").bitcast(I32))
        lb_t = load_list("lb_t", lb)
        la_t = load_list("la_t", la)

        x_scale_picked = sb.tile([P, S], U8, name="x_scale_picked", align_bytes=64)
        nc.vector.tensor_copy(x_scale_picked[:], x_scale_table[:].indirect(offs_t[:]))

        w1_bf = [
            shared.tile([P, 2 * PACK * P], BF16, name="w1_bf_early", offset=2048, align_bytes=64),
            sb.tile([P, 2 * PACK * P], BF16, name="w1_bf_late", tag="w1_bf_late", align_bytes=64),
        ]
        source = w1_raw[:].rearrange("p j (m t) -> p m t j", t=PACK)
        dealt = [tile[:].rearrange("p (t m j) -> p m t j", t=2, j=PACK) for tile in w1_bf]
        nc.vector.tensor_copy(out=dealt[0], in_=source[:, :, 0:2, :])
        nc.scalar.activation(dealt[1], source[:, :, 2:4, :], COPY)
        w1_codes = [
            sb.tile([P, 2 * P], U32, name="w1_codes_early", align_bytes=64),
            shared.tile([P, 2 * P], U32, name="w1_codes_late", offset=4096 + 1024, align_bytes=64),
        ]
        w1_scales = [sb.tile([P, 2 * P], U8, name="w1_scales%d" % u, align_bytes=64) for u in range(2)]
        nc.vector.quantize_mx(out=w1_codes[0][:].bitcast(FP8X4), scales=w1_scales[0][:], in_=w1_bf[0][:])

        w2_raw = sb.tile([P, 2 * N], U8, name="w2_raw", tag="w1_raw", align_bytes=64)
        nc.sync.dma_start(out=w2_raw[:].bitcast(I32), in_=w2_words[0].bitcast(I32))

        x_picked = shared.tile([P, S], U32, name="x_picked", offset=1024, align_bytes=64)
        for h in range(2):
            nc.vector.tensor_copy(
                x_picked[:, h * HALF : (h + 1) * HALF],
                x_table[:].indirect(offs_t[:, h * HALF // 16 : (h + 1) * HALF // 16]),
            )

        nc.vector.quantize_mx(out=w1_codes[1][:].bitcast(FP8X4), scales=w1_scales[1][:], in_=w1_bf[1][:])

        y = [sb.tile([P, S], F32, name="y%d" % t, align_bytes=64) for t in range(PACK)]

        def first_product(t, cols, tag):
            rows = slice(t % 2 * P, (t % 2 + 1) * P)
            bank = psum.tile([P, cols.stop - cols.start], F32, name="bank_" + tag, tag=tag)
            nc.tensor.matmul_mx(
                out=bank[:],
                lhsT=w1_codes[t // 2][:, rows].bitcast(FP8X4),
                lhsT_scale=w1_scales[t // 2][:, rows],
                rhs=x_picked[:, cols].bitcast(FP8X4),
                rhs_scale=x_scale_picked[:, cols],
                start=True,
                stop=True,
            )
            nc.scalar.copy(y[t][:, cols], bank[:])

        first_product(0, slice(0, HALF), "b0")
        first_product(0, slice(HALF, S), "b1")
        for t in range(1, PACK):
            first_product(t, slice(0, S), "b%d" % (t + 1))

        w2_scale_raw = sb.tile([P, N], U8, name="w2_scale_raw", tag="w1_bf_late", align_bytes=64)
        nc.gpsimd.memset(w2_scale_raw[:].bitcast(I32), 0)
        load_scale_rows(nc.sync, w2_scale_raw, w2_scales[0])
        w2_codes = shared.tile([P, 2 * N], U8, name="w2_codes", offset=4096, align_bytes=64)
        nc.vector.tensor_copy(
            out=w2_codes[:].rearrange("p (t m b) -> p t m b", t=PACK, b=2),
            in_=w2_raw[:].rearrange("p (m t b) -> p t m b", t=PACK, b=2),
        )

        def small(name, t):
            return sb.tile([P, V], F32, name="%s%d" % (name, t), tag="%s%d" % (name, t), align_bytes=64)

        fetched = sb.tile([P, 4 * PACK * V], F32, name="fetched", tag="w1_raw", align_bytes=64)
        a, b, c, d = ([fetched[:, (4 * t + k) * V : (4 * t + k + 1) * V] for t in range(PACK)] for k in range(4))
        minus_c = [small("minus_c", t) for t in range(PACK)]
        larger = [small("larger", t) for t in range(PACK)]
        smaller = [small("smaller", t) for t in range(PACK)]
        z = [sb.tile([P, S], F32, name="z%d" % t, align_bytes=64) for t in range(PACK)]
        z_bf = [sb.tile([P, CHUNK, PACK], BF16, name="z_bf%d" % i, align_bytes=64) for i in range(CHUNKS)]

        def gathers(t):
            return [
                lambda: nc.vector.tensor_copy(c[t], y[t][:].indirect(lc_t[:])),
                lambda: nc.vector.tensor_copy(d[t], y[t][:].indirect(ld_t[:])),
                lambda: nc.vector.tensor_copy(b[t], y[t][:].indirect(lb_t[:])),
                lambda: nc.vector.tensor_copy(a[t], y[t][:].indirect(la_t[:])),
            ]

        def scatters(t):
            return [
                lambda: nc.vector.tensor_tensor(z[t][:].indirect(lc_t[:]), c[t], d[t], ALU.add),
                lambda: nc.vector.tensor_copy(z[t][:].indirect(ld_t[:]), smaller[t][:]),
                lambda: nc.vector.tensor_copy(z[t][:].indirect(lb_t[:]), larger[t][:]),
                lambda: nc.vector.tensor_tensor(z[t][:].indirect(la_t[:]), a[t], minus_c[t][:], ALU.add),
            ]

        def round_z(t, i, on_vector):
            src = z[t][:, i * CHUNK : (i + 1) * CHUNK]
            if on_vector:
                nc.vector.tensor_copy(z_bf[i][:, :, t], src)
            else:
                nc.scalar.copy(z_bf[i][:, :, t], src)

        for t in range(PACK):
            put = scatters(t - 1) if t > 0 else None
            for k, fetch in enumerate(gathers(t)):
                fetch()
                if k == 0:
                    nc.scalar.activation(minus_c[t][:], c[t], COPY, scale=-1.0)
                if put:
                    put[k]()
            nc.vector.tensor_tensor(smaller[t][:], b[t], d[t], ALU.min)
            nc.vector.tensor_tensor(larger[t][:], a[t], b[t], ALU.max)
            if t in (1, 2):
                for i in range(CHUNKS):
                    round_z(t - 1, i, False)
        last = scatters(PACK - 1)
        round_z(2, 2, False)
        round_z(2, 3, False)
        last[0]()
        round_z(2, 0, True)
        last[1]()
        round_z(2, 1, True)
        last[2]()
        w2_scale = sb.tile([P, N], U8, name="w2_scale", tag="smaller3", align_bytes=64)
        nc.vector.tensor_copy(
            out=w2_scale[:].rearrange("p (t m) -> p t m", t=PACK),
            in_=w2_scale_raw[:].rearrange("p (m t) -> p t m", t=PACK),
        )
        last[3]()
        for i in range(CHUNKS):
            round_z(3, i, i < 2)

        z_codes = sb.tile([P, S], U32, name="z_codes", align_bytes=64)
        z_scales = sb.tile([P, S], U8, name="z_scales", align_bytes=64)
        for i in range(CHUNKS):
            cols = slice(i * CHUNK, (i + 1) * CHUNK)
            nc.vector.quantize_mx(
                out=z_codes[:, cols].bitcast(FP8X4),
                scales=z_scales[:, cols],
                in_=z_bf[i][:].rearrange("p n t -> p (n t)"),
            )

        out_rows = out_0.rearrange("(p t) n -> p t n", t=PACK)
        out_words = out_1[0].rearrange("p n t -> p (n t)").bitcast(I32)
        out_codes = sb.tile([P, S], U32, name="out_codes", align_bytes=64)
        out_scales = sb.tile([P, S], U8, name="out_scales", align_bytes=64)
        first_half = sb.tile([P, HALF * PACK], BF16, name="first_half", align_bytes=64)
        third = sb.tile([P, CHUNK * PACK], BF16, name="third", align_bytes=64)
        fourth = sb.tile([P, CHUNK * PACK], BF16, name="fourth", align_bytes=64)
        result_bf = [first_half[:, : CHUNK * PACK], first_half[:, CHUNK * PACK :], third[:], fourth[:]]

        def quantize_result(values, cols):
            nc.vector.quantize_mx(out=out_codes[:, cols].bitcast(FP8X4), scales=out_scales[:, cols], in_=values)

        for i in range(CHUNKS):
            cols = slice(i * CHUNK, (i + 1) * CHUNK)
            result = sb.tile([P, PACK, CHUNK], F32, name="result%d" % i, align_bytes=64)
            for u in range(2):
                tag = "b%d" % ((2 * i + u + 5) % 8)
                bank = psum.tile([P, 2, CHUNK], F32, name="out_bank%d_%d" % (i, u), tag=tag)
                for e in range(2):
                    t = 2 * u + e
                    nc.tensor.matmul_mx(
                        out=bank[:, e, :],
                        lhsT=w2_codes[:, 2 * t * P : 2 * (t + 1) * P].bitcast(FP4X4),
                        lhsT_scale=w2_scale[:, t * P : (t + 1) * P],
                        rhs=z_codes[:, cols].bitcast(FP8X4),
                        rhs_scale=z_scales[:, cols],
                        start=True,
                        stop=True,
                    )
                pair = slice(2 * u, 2 * u + 2)
                if (i, u) == (0, 1):
                    nc.vector.tensor_copy(result[:, pair, :], bank[:])
                else:
                    nc.scalar.copy(result[:, pair, :], bank[:])
                if i == 0:
                    nc.sync.dma_start(out=out_rows[:, pair, cols], in_=result[:, pair, :])
            if i > 0:
                nc.sync.dma_start(out=out_rows[:, :, cols], in_=result[:])
            nc.vector.tensor_copy(
                out=result_bf[i].rearrange("p (n i t) -> p n t i", i=4, t=PACK),
                in_=result[:].rearrange("p t (n i) -> p n t i", i=4),
            )
            if i == 2:
                quantize_result(first_half[:], slice(0, HALF))
        for i in (2, 3):
            quantize_result(result_bf[i], slice(i * CHUNK, (i + 1) * CHUNK))
        for cols in (slice(0, 3 * CHUNK), slice(3 * CHUNK, S)):
            nc.sync.dma_start(out=out_words[:, cols], in_=out_codes[:, cols].bitcast(I32))
        for q in range(QUADS):
            engine = nc.sync if q % 2 == 0 else nc.scalar
            engine.dma_start(
                out=out_2[0][4 * q : 4 * q + 4, :].bitcast(I32),
                in_=out_scales[32 * q : 32 * q + 4, :].bitcast(I32),
            )
